import numpy as np
import ml_dtypes


def mxq(x, axis, fmt="e4m3"):
    dtype, down = {"e4m3": (ml_dtypes.float8_e4m3fn, 7), "e5m2": (ml_dtypes.float8_e5m2, 14)}[fmt]
    v = np.moveaxis(np.asarray(x, np.float32).astype(ml_dtypes.bfloat16).astype(np.float64), axis, -1)
    blocks = v.reshape(v.shape[:-1] + (-1, 32))
    amax = np.abs(blocks).max(-1, keepdims=True)
    byte = np.maximum(np.where(amax > 0, np.frexp(amax)[1] - 1 + 127, 0) - down, 1)
    scale = np.exp2(byte - 127.0)
    codes = (blocks / scale).astype(np.float32).astype(dtype).astype(np.float64)
    return np.moveaxis((codes * scale).reshape(v.shape), -1, axis)


WIDE = False


def mx_kscale(k):
    if not WIDE:
        return np.ones(k)
    levels = np.array([10, -10, 5, -5, 0])
    if k % 512:
        return np.exp2(np.random.permutation(np.resize(levels, k // 32))).repeat(32)
    a = np.empty((k // 512, 16))
    for p in range(k // 512):
        a[p, :8] = np.random.permutation(np.resize(levels, 8))
        for g in range(8):
            far = levels[np.abs(levels - a[p, g]) >= 10]
            a[p, g + 8] = far[np.random.randint(len(far))]
    return np.exp2(a.ravel()).repeat(32)


def f64(x):
    return np.asarray(x).astype(np.float64)


def striped(idx):
    return np.tile(idx.reshape(-1, 16).T, (8, 1)).astype(np.uint16)


def unstriped(offs):
    return offs[:16].T.reshape(-1).astype(np.int64)


E2M1 = np.array([0.0, 0.5, 1.0, 1.5, 2.0, 3.0, 4.0, 6.0, -0.0, -0.5, -1.0, -1.5, -2.0, -3.0, -4.0, -6.0])


def pack_weight(w, fmt):
    k, n = w.shape
    w = f64(np.asarray(w, np.float32).astype(ml_dtypes.bfloat16)).reshape(k // 32, 32, n)
    amax = np.abs(w).max(1)
    if fmt == "e4m3":
        byte = np.frexp(amax)[1] - 1 + 127 - 7
    else:
        mant, ex = np.frexp(amax / 6.0)
        byte = np.where(mant > 0.5, ex, ex - 1) + 127
    byte = np.clip(np.where(amax > 0, byte, 1), 1, 254)
    scaled = (w * np.exp2(127.0 - byte)[:, None, :]).reshape(k, n).astype(np.float32)
    by_word = np.ascontiguousarray(scaled.reshape(k // 512, 128, 4, n).transpose(0, 1, 3, 2))
    if fmt == "e4m3":
        words = by_word.astype(ml_dtypes.float8_e4m3fn).view(np.uint8)
    else:
        c = by_word.astype(ml_dtypes.float4_e2m1fn).view(np.uint8) & 0xF
        words = (c[..., 0::2] | (c[..., 1::2] << 4)).reshape(k // 512, 128, 2 * n)
    return np.ascontiguousarray(words), np.ascontiguousarray(byte.astype(np.uint8).reshape(k // 512, 16, n))


def unpack_weight(words, scales, fmt):
    g, _, n = scales.shape
    words = np.ascontiguousarray(words).reshape(g, 128, n, -1)
    if fmt == "e4m3":
        vals = words.view(ml_dtypes.float8_e4m3fn).astype(np.float64)
    else:
        nib = np.empty((g, 128, n, 4), np.uint8)
        nib[..., 0::2] = words & 0xF
        nib[..., 1::2] = words >> 4
        vals = E2M1[nib]
    vals = vals * np.repeat(np.exp2(scales.astype(np.float64) - 127.0), 8, axis=1)[..., None]
    return vals.transpose(0, 1, 3, 2).reshape(g * 512, n)


def relu(v):
    return np.maximum(v, 0.0)


K, T, Q, E, C, D, H = 1024, 512, 512, 4, 256, 256, 512
N = 256


def by_expert(wq, xq, C):
    return np.concatenate([wq[e].T @ xq[:, e * C:(e + 1) * C] for e in range(E)], axis=1)


def setup_inputs():
    n = np.random.standard_normal
    s = mx_kscale(K)
    u = mx_kscale(H)
    first = np.random.permutation(np.repeat(np.arange(E), T // E))
    second = (first + 1 + np.random.permutation(np.repeat(np.arange(E - 1), -(-T // (E - 1)))[:T])) % E
    while np.bincount(second, minlength=E).max() != T // E:
        load = np.bincount(second, minlength=E); hi, lo = int(load.argmax()), int(load.argmin())
        t = np.flatnonzero((second == hi) & (first != lo))[0]; second[t] = lo
    slot_token = np.empty(E * C, np.int64); pos = np.empty((2, T), np.int64); fill = np.zeros(E, np.int64)
    place = np.stack([np.random.permutation(C) for _ in range(E)])
    for r, deal in enumerate((first, second)):
        for t in np.random.permutation(T):
            e = deal[t]; j = e * C + place[e, fill[e]]; fill[e] += 1; slot_token[j] = t; pos[r, t] = j
    g = np.random.uniform(0.2, 0.8, T)
    slots2 = np.concatenate([np.random.permutation(Q)[:D] for e in range(E)])
    x = pack_weight(n((K, Q)) * s[:, None], "e4m3")
    return {
        "x_words": x[0],
        "x_scales": x[1],
        "xo": (n((K, T)) * s[:, None]).astype(np.float32),
        "w1": (n((E, K, H)) / np.sqrt(K) / s[None, :, None] * u).astype(np.float32),
        "w2": (n((E, H, N)) / np.sqrt(H) / u[None, :, None]).astype(np.float32),
        "gate": np.stack([np.tile(g, (128, 1)), np.tile(1.0 - g, (128, 1))]).astype(np.float32),
        "offs": striped(slot_token),
        "pos1": striped(pos[0]),
        "pos2": striped(pos[1]),
        "offs2": striped(slots2),
    }


def reference(x_words, x_scales, xo, w1, w2, gate, offs, pos1, pos2, offs2):
    w1q = mxq(f64(w1), 1, "e4m3")
    w2q = mxq(f64(w2), 1, "e4m3")
    idx, idx2 = unstriped(offs), unstriped(offs2)
    xq = mxq(f64(xo)[:, idx], 0, "e4m3")
    rq = unpack_weight(x_words, x_scales, "e4m3")[:, idx2]
    h = relu(by_expert(w1q, xq, C))
    y = by_expert(w2q, mxq(h, 0, "e4m3"), C)
    h = relu(by_expert(w1q, rq, D))
    z = by_expert(w2q, mxq(h, 0, "e4m3"), D)
    own = sum(f64(gate[r, :1]) * y[:, unstriped(p)] for r, p in enumerate((pos1, pos2)))
    return np.concatenate([own, z], axis=1)

@@ -1,0 +1,216 @@
+from contextlib import ExitStack
+
+import concourse.mybir as mybir
+
+K, T, Q, E, C, D, H, N = 1024, 512, 512, 4, 256, 256, 512, 256
+FLOPS = 2 * E * (C + D) * (K * H + H * N)
+
+F32 = mybir.dt.float32
+BF16 = mybir.dt.bfloat16
+I32 = mybir.dt.int32
+U32 = mybir.dt.uint32
+U16 = mybir.dt.uint16
+U8 = mybir.dt.uint8
+FP8X4 = mybir.dt.float8_e4m3fn_x4
+RELU = mybir.ActivationFunctionType.Relu
+MULT = mybir.AluOpType.mult
+ADD = mybir.AluOpType.add
+
+P = 128
+PACK = 4
+K_PASS = P * PACK
+PASSES = K // K_PASS
+LIST_COLS = C // 16
+N_TILES = N // P
+PICKED_SLOT = [None, None, "w1_grouped01", "w1_grouped11"]
+FAR_WORD_SLOT = ["own_grouped0", "own_grouped1", "w1_grouped21", "own_grouped3"]
+FAR_SCALE_SLOT = ["w1_grouped00", "w1_grouped10", "w2_grouped2", "w2_grouped3"]
+
+
+def tile_moe_loc_mlp_relu_kernel(tc, x_words, x_scales, xo, w1, w2, gate, offs, pos1, pos2, offs2, out):
+    nc = tc.nc
+    with ExitStack() as ctx:
+        lists = ctx.enter_context(tc.tile_pool(name="lists", bufs=1))
+        keep = ctx.enter_context(tc.tile_pool(name="keep", bufs=1))
+        psum = ctx.enter_context(tc.psum_pool(name="psum", bufs=1))
+
+        def held(shape, dtype, name, bufs=1, slot=None):
+            return keep.tile(shape, dtype, name=name, tag=slot or name, align_bytes=64, bufs=bufs)
+
+        offs_sb = lists.tile([P, E * LIST_COLS], U16, name="offs_sb")
+        offs2_sb = lists.tile([P, E * LIST_COLS], U16, name="offs2_sb")
+        pos_sb = [lists.tile([P, T // 16], U16, name=f"pos_sb{r}") for r in range(2)]
+
+        zero = held([P, 1], F32, "zero")
+        no_bias = held([P, 1], F32, "no_bias")
+        nc.vector.memset(zero[:], 0.0)
+        nc.scalar.activation(out=no_bias[:], in_=zero[:], func=RELU)
+
+        far_scales = held([P, Q // 4], I32, "far_scales")
+        nc.vector.memset(far_scales[:], 0)
+
+        far_words = [held([P, Q], I32, f"far_words{s}") for s in range(PASSES)]
+        xo_raw = {}
+        w1_raw = {}
+        w2_raw = {}
+
+        def load_far_words(s):
+            nc.sync.dma_start(out=far_words[s][:], in_=x_words[s].rearrange("p t d -> p (t d)").bitcast(I32))
+
+        def load_xo(s, u):
+            xo_raw[s, u] = held([P, 2, T], F32, f"xo_raw{s}{u}")
+            rows = xo[s * K_PASS : (s + 1) * K_PASS, :].rearrange("(p j) t -> p j t", j=PACK)
+            nc.sync.dma_start(out=xo_raw[s, u][:], in_=rows[:, 2 * u : 2 * u + 2, :])
+
+        def load_w1(e, s):
+            w1_raw[e, s] = held([P, PACK, H], F32, f"w1_raw{e}{s}")
+            rows = w1[e, s * K_PASS : (s + 1) * K_PASS, :].rearrange("(p j) h -> p j h", j=PACK)
+            nc.sync.dma_start(out=w1_raw[e, s][:], in_=rows)
+
+        def load_w2(e):
+            w2_raw[e] = held([P, PACK, N], F32, f"w2_raw{e}")
+            nc.sync.dma_start(out=w2_raw[e][:], in_=w2[e].rearrange("(p j) n -> p j n", j=PACK))
+
+        nc.sync.dma_start(offs2_sb[:], offs2)
+        load_far_words(0)
+        nc.sync.dma_start(offs_sb[:], offs)
+        for s in range(PASSES):
+            for u in range(2):
+                load_xo(s, u)
+        for quad in range(4):
+            nc.sync.dma_start(
+                out=far_scales[32 * quad : 32 * quad + 4 * PASSES, :],
+                in_=x_scales[:, 4 * quad : 4 * quad + 4, :].bitcast(I32),
+            )
+        load_w1(0, 0)
+        load_w1(0, 1)
+        load_far_words(1)
+        for e in range(1, E):
+            load_w1(e, 0)
+            load_w2(e - 1)
+            load_w1(e, 1)
+        load_w2(E - 1)
+        nc.sync.dma_start(pos_sb[0][:], pos1)
+        nc.sync.dma_start(pos_sb[1][:], pos2)
+        gate_sb = held([P, 2, T], F32, "gate_sb")
+        nc.sync.dma_start(out=gate_sb[:], in_=gate.rearrange("r p t -> p r t"))
+
+        pairs = {}
+        for s in range(PASSES):
+            for u in range(2):
+                pairs[s, u] = held([P, T, 2], BF16, f"pairs{s}{u}")
+                nc.scalar.copy(out=pairs[s, u][:], in_=xo_raw[s, u][:].rearrange("p j t -> p t j"))
+
+        def quantize(values, width, name):
+            codes = held([P, width], U32, name + "_codes")
+            scales = held([P, width], U8, name + "_scales")
+            nc.vector.quantize_mx(out=codes[:].bitcast(FP8X4), scales=scales[:], in_=values)
+            return codes, scales
+
+        def expert_list(tile, e):
+            return tile[:, e * LIST_COLS : (e + 1) * LIST_COLS]
+
+        def own_tokens(e):
+            picked = held([P, 2, PASSES * C], U32, f"picked{e}", slot=PICKED_SLOT[e])
+            for s in range(PASSES):
+                for u in range(2):
+                    window = pairs[s, u][:].rearrange("p t j -> p (t j)").bitcast(U32)
+                    nc.vector.tensor_copy(picked[:, u, s * C : (s + 1) * C], window.indirect(expert_list(offs_sb, e)))
+            grouped = held([P, PASSES * C * PACK], BF16, f"own_grouped{e}")
+            nc.vector.tensor_copy(
+                out=grouped[:].bitcast(I32).rearrange("p (c u) -> p c u", u=2),
+                in_=picked[:].bitcast(I32).rearrange("p u c -> p c u"),
+            )
+            codes, scales = quantize(grouped[:], PASSES * C, f"own{e}")
+            return [(codes[:, s * C : (s + 1) * C], scales[:, s * C : (s + 1) * C]) for s in range(PASSES)]
+
+        def far_tokens(e):
+            scales = held([P, D], U8, f"far_picked_scales{e}", slot=FAR_SCALE_SLOT[e])
+            nc.vector.tensor_copy(scales[:], far_scales[:].bitcast(U8).indirect(expert_list(offs2_sb, e)))
+            operands = []
+            for s in range(PASSES):
+                words = held([P, D], U32, f"far_picked_words{e}{s}", slot=FAR_WORD_SLOT[e] if s else None)
+                nc.vector.tensor_copy(words[:], far_words[s][:].bitcast(U32).indirect(expert_list(offs2_sb, e)))
+                operands.append((words[:], scales[4 * s : P, :]))
+            return operands
+
+        def first_matrix(e):
+            operands = []
+            for s in range(PASSES):
+                grouped = held([P, H * PACK], BF16, f"w1_grouped{e}{s}", slot=f"w1_grouped{e % 2 if s == 0 else e}{s}")
+                nc.scalar.copy(
+                    out=grouped[:].rearrange("p (t m j) -> p m j t", t=PACK, j=PACK),
+                    in_=w1_raw[e, s][:].rearrange("p j (m t) -> p m j t", t=PACK),
+                )
+                operands.append(quantize(grouped[:], H, f"w1_{e}{s}"))
+            return operands
+
+        def second_matrix(e):
+            grouped = held([P, N * PACK], BF16, f"w2_grouped{e}")
+            nc.vector.tensor_copy(
+                out=grouped[:].rearrange("p (c i j) -> p c j i", i=4, j=PACK),
+                in_=w2_raw[e][:].rearrange("p j (c i) -> p c j i", i=4),
+            )
+            return quantize(grouped[:], N, f"w2_{e}")
+
+        def expert(tokens, first, second, kind, e, h_bufs, y_bufs):
+            hidden = held([P, C, PACK], BF16, f"hidden_{kind}", 2)
+            for half in range(C // P):
+                slots = slice(half * P, (half + 1) * P)
+                bank = psum.tile([P, PACK, P], F32, name=f"h_{kind}", bufs=h_bufs)
+                for t in range(PACK):
+                    cols = slice(t * P, (t + 1) * P)
+                    for s in range(PASSES):
+                        nc.tensor.matmul_mx(
+                            out=bank[:, t, :],
+                            lhsT=first[s][0][:, cols].bitcast(FP8X4),
+                            lhsT_scale=first[s][1][:, cols],
+                            rhs=tokens[s][0][:, slots].bitcast(FP8X4),
+                            rhs_scale=tokens[s][1][:, slots],
+                            start=(s == 0),
+                            stop=(s == PASSES - 1),
+                        )
+                nc.scalar.activation(
+                    out=hidden[:, slots, :], in_=bank[:].rearrange("p t c -> p c t"), func=RELU, bias=no_bias[:]
+                )
+            codes, scales = quantize(hidden[:].rearrange("p c t -> p (c t)"), C, f"h_{kind}{e}")
+            sums = psum.tile([P, N_TILES, C], F32, name=f"y_{kind}", bufs=y_bufs)
+            for nt in range(N_TILES):
+                cols = slice(nt * P, (nt + 1) * P)
+                nc.tensor.matmul_mx(
+                    out=sums[:, nt, :],
+                    lhsT=second[0][:, cols].bitcast(FP8X4),
+                    lhsT_scale=second[1][:, cols],
+                    rhs=codes[:].bitcast(FP8X4),
+                    rhs_scale=scales[:],
+                    start=True,
+                    stop=True,
+                )
+            return sums
+
+        out_rows = out.rearrange("(nt p) c -> p nt c", p=P)
+        slot_rows = [held([P, E * C], F32, f"slot_rows{nt}") for nt in range(N_TILES)]
+        firsts, seconds = [], []
+        for e in range(E):
+            tokens = own_tokens(e)
+            firsts.append(first_matrix(e))
+            seconds.append(second_matrix(e))
+            sums = expert(tokens, firsts[e], seconds[e], "own", e, 3, 2)
+            for nt in range(N_TILES):
+                nc.scalar.copy(out=slot_rows[nt][:, e * C : (e + 1) * C], in_=sums[:, nt, :])
+
+        for e in range(E):
+            sums = expert(far_tokens(e), firsts[e], seconds[e], "far", e, 2, 1)
+            result = held([P, N_TILES, D], F32, f"far_result{e}", slot=f"w1_raw{1 + e // 2}{e % 2}")
+            nc.scalar.copy(out=result[:], in_=sums[:])
+            nc.sync.dma_start(out=out_rows[:, :, T + e * D : T + (e + 1) * D], in_=result[:])
+
+        for nt in range(N_TILES):
+            parts = []
+            for r in range(2):
+                part = held([P, T], F32, f"part{nt}{r}", slot=f"xo_raw{nt}{r}")
+                nc.vector.tensor_tensor(part[:], slot_rows[nt][:].indirect(pos_sb[r][:]), gate_sb[:, r, :], MULT)
+                parts.append(part)
+            combined = held([P, T], F32, f"combined{nt}", slot=f"w1_raw0{nt}")
+            nc.vector.tensor_tensor(combined[:], parts[0][:], parts[1][:], ADD)
+            nc.sync.dma_start(out=out_rows[:, nt, 0:T], in_=combined[:])

@@ -22,9 +22,137 @@ K_PASS = P * PACK
 PASSES = K // K_PASS
 LIST_COLS = C // 16
 N_TILES = N // P
-PICKED_SLOT = [None, None, "w1_grouped01", "w1_grouped11"]
-FAR_WORD_SLOT = ["own_grouped0", "own_grouped1", "w1_grouped21", "own_grouped3"]
-FAR_SCALE_SLOT = ["w1_grouped00", "w1_grouped10", "w2_grouped2", "w2_grouped3"]
+
+SLOT = {
+    "part00": "xo_raw00",
+    "part01": "xo_raw01",
+    "part10": "xo_raw10",
+    "part11": "xo_raw11",
+    "combined0": "picked0",
+    "combined1": "picked1",
+    "far_s1": "w1_raw11",
+    "hidden_own2": "w1_raw31",
+    "far_result2": "w1_raw11",
+    "far_result3": "w1_raw21",
+    "hidden_own0": "w1_grouped11",
+    "hidden_own1": "w2_grouped0",
+    "hidden_far1": "w2_raw1",
+    "far_result0": "w1_raw00",
+    "w1_grouped31": "w1_raw11",
+    "own_grouped2": "w1_raw20",
+    "hidden_own3": "w2_grouped0",
+    "hidden_far2": "w1_raw20",
+    "w2_grouped1": "w1_raw00",
+    "own_grouped0": "w1_grouped21",
+    "own_grouped3": "xo_raw11",
+    "hidden_far3": "xo_raw11",
+    "w1_grouped30": "xo_raw10",
+    "far_result1": "own_grouped1",
+}
+
+LOADS = [("Lfw", 1), ("Llist", "offs2"), ("Lxo", 1, 1), ("Lxo", 1, 0), ("Llist", "offs"), ("Lxo", 0, 1), ("Lxo", 0, 0), ("Lw1", 0, 0), ("Lw1", 0, 1), ("Lw1", 1, 0), ("Llist", "pos1"), ("Lw1", 1, 1), ("Lw1", 2, 0), ("Lfw", 0), ("Lfs",), ("Lw1", 2, 1), ("Lw2", 0), ("Lw1", 3, 0), ("Lgate",), ("Llist", "pos0"), ("Lw1", 3, 1), ("Lw2", 1), ("Lw2", 2), ("Lw2", 3)]
+ORDER = [
+    ("fw", 0, 1),
+    ("fw", 0, 0),
+    ("c1", 0, 0, 0),
+    ("c2", 0),
+    ("c1", 0, 0, 1),
+    ("c1", 0, 1, 0),
+    ("cx", 1, 1),
+    ("og", 0, 1, 1),
+    ("c2", 1),
+    ("q1", 0, 0),
+    ("cx", 1, 0),
+    ("c1", 0, 1, 1),
+    ("cx", 0, 1),
+    ("og", 0, 1, 0),
+    ("il", 1),
+    ("q2", 0),
+    ("qo", 1),
+    ("q2", 1),
+    ("cx", 0, 0),
+    ("c2", 2),
+    ("og", 0, 0, 1),
+    ("og", 0, 0, 0),
+    ("q2", 2),
+    ("og", 1, 1, 1),
+    ("q1", 0, 1),
+    ("og", 1, 1, 0),
+    ("c1", 1, 0, 0),
+    ("il", 0),
+    ("c1", 1, 0, 1),
+    ("c2", 3),
+    ("il", 3),
+    ("c1", 1, 1, 0),
+    ("c1", 1, 1, 1),
+    ("q1", 1, 0),
+    ("c1", 2, 0, 0),
+    ("c1", 2, 0, 1),
+    ("qo", 0),
+    ("q1", 1, 1),
+    ("og", 1, 0, 1),
+    ("c1", 2, 1, 0),
+    ("q1", 2, 0),
+    ("c1", 2, 1, 1),
+    ("h", "own", 0, 0),
+    ("h", "own", 0, 1),
+    ("og", 1, 0, 0),
+    ("c1", 3, 0, 0),
+    ("il", 2),
+    ("fs", 0),
+    ("h", "own", 1, 0),
+    ("qo", 3),
+    ("qh", "own", 0),
+    ("c1", 3, 0, 1),
+    ("q1", 2, 1),
+    ("h", "own", 1, 1),
+    ("qh", "own", 1),
+    ("h", "far", 0, 0),
+    ("c1", 3, 1, 0),
+    ("h", "far", 0, 1),
+    ("qh", "far", 0),
+    ("q1", 3, 0),
+    ("c1", 3, 1, 1),
+    ("y", "own", 0),
+    ("qo", 2),
+    ("h", "own", 2, 0),
+    ("q1", 3, 1),
+    ("h", "own", 2, 1),
+    ("fw", 1, 1),
+    ("h", "far", 1, 0),
+    ("h", "own", 3, 0),
+    ("h", "own", 3, 1),
+    ("fs", 1),
+    ("fw", 1, 0),
+    ("q2", 3),
+    ("h", "far", 1, 1),
+    ("h", "far", 2, 0),
+    ("qh", "own", 2),
+    ("y", "own", 1),
+    ("qh", "own", 3),
+    ("y", "far", 0),
+    ("y", "own", 2),
+    ("h", "far", 2, 1),
+    ("y", "own", 3),
+    ("h", "far", 3, 0),
+    ("h", "far", 3, 1),
+    ("qh", "far", 1),
+    ("y", "far", 1),
+    ("qh", "far", 2),
+    ("cg", 1, 0),
+    ("cg", 0, 1),
+    ("qh", "far", 3),
+    ("cg", 1, 1),
+    ("y", "far", 2),
+    ("add", 1),
+    ("cg", 0, 0),
+    ("y", "far", 3),
+    ("add", 0),
+]
+W1_ENGINE = {(3, 0, 0): "vector", (3, 0, 1): "vector", (3, 1, 0): "vector"}
+W2_ENGINE = ["scalar", "vector", "vector", "vector"]
+XO_ENGINE = ["scalar", "scalar", "scalar", "scalar"]
+Z_ON_VECTOR = [0]
 
 
 def tile_moe_loc_mlp_relu_kernel(tc, x_words, x_scales, xo, w1, w2, gate, offs, pos1, pos2, offs2, out):
@@ -34,8 +162,8 @@ def tile_moe_loc_mlp_relu_kernel(tc, x_words, x_scales, xo, w1, w2, gate, offs, 
         keep = ctx.enter_context(tc.tile_pool(name="keep", bufs=1))
         psum = ctx.enter_context(tc.psum_pool(name="psum", bufs=1))
 
-        def held(shape, dtype, name, bufs=1, slot=None):
-            return keep.tile(shape, dtype, name=name, tag=slot or name, align_bytes=64, bufs=bufs)
+        def held(shape, dtype, name):
+            return keep.tile(shape, dtype, name=name, tag=SLOT.get(name, name), align_bytes=64)
 
         offs_sb = lists.tile([P, E * LIST_COLS], U16, name="offs_sb")
         offs2_sb = lists.tile([P, E * LIST_COLS], U16, name="offs2_sb")
@@ -46,16 +174,25 @@ def tile_moe_loc_mlp_relu_kernel(tc, x_words, x_scales, xo, w1, w2, gate, offs, 
         nc.vector.memset(zero[:], 0.0)
         nc.scalar.activation(out=no_bias[:], in_=zero[:], func=RELU)
 
-        far_scales = held([P, Q // 4], I32, "far_scales")
+        far_scales = held([P, 2 * Q // 4], I32, "far_scales")
         nc.vector.memset(far_scales[:], 0)
 
-        far_words = [held([P, Q], I32, f"far_words{s}") for s in range(PASSES)]
-        xo_raw = {}
-        w1_raw = {}
-        w2_raw = {}
+        far_words = held([P, (PASSES + 1) * Q], I32, "far_words")
+        nc.vector.memset(far_words[:, PASSES * Q :], 0)
+        pair_words = held([P, (2 * PASSES + 1) * T], I32, "pair_words")
+        nc.vector.memset(pair_words[:, 2 * PASSES * T :], 0)
+        gate_sb = held([P, 2, T], F32, "gate_sb")
+        xo_raw, w1_raw, w2_raw = {}, {}, {}
 
         def load_far_words(s):
-            nc.sync.dma_start(out=far_words[s][:], in_=x_words[s].rearrange("p t d -> p (t d)").bitcast(I32))
+            nc.sync.dma_start(out=far_words[:, s * Q : (s + 1) * Q], in_=x_words[s].rearrange("p t d -> p (t d)").bitcast(I32))
+
+        def load_far_scales():
+            for quad in range(4):
+                nc.sync.dma_start(
+                    out=far_scales[32 * quad : 32 * quad + 4 * PASSES, 0 : Q // 4],
+                    in_=x_scales[:, 4 * quad : 4 * quad + 4, :].bitcast(I32),
+                )
 
         def load_xo(s, u):
             xo_raw[s, u] = held([P, 2, T], F32, f"xo_raw{s}{u}")
@@ -69,37 +206,42 @@ def tile_moe_loc_mlp_relu_kernel(tc, x_words, x_scales, xo, w1, w2, gate, offs, 
 
         def load_w2(e):
             w2_raw[e] = held([P, PACK, N], F32, f"w2_raw{e}")
-            nc.sync.dma_start(out=w2_raw[e][:], in_=w2[e].rearrange("(p j) n -> p j n", j=PACK))
+            rows = w2[e].rearrange("(c a i b) n -> a c i (b n)", a=2, i=2, b=2)
+            for a in range(2):
+                nc.sync.dma_start(out=w2_raw[e][:, 2 * a : 2 * a + 2, :].rearrange("p b n -> p (b n)"), in_=rows[a])
 
-        nc.sync.dma_start(offs2_sb[:], offs2)
-        load_far_words(0)
-        nc.sync.dma_start(offs_sb[:], offs)
-        for s in range(PASSES):
-            for u in range(2):
-                load_xo(s, u)
-        for quad in range(4):
-            nc.sync.dma_start(
-                out=far_scales[32 * quad : 32 * quad + 4 * PASSES, :],
-                in_=x_scales[:, 4 * quad : 4 * quad + 4, :].bitcast(I32),
-            )
-        load_w1(0, 0)
-        load_w1(0, 1)
-        load_far_words(1)
-        for e in range(1, E):
-            load_w1(e, 0)
-            load_w2(e - 1)
-            load_w1(e, 1)
-        load_w2(E - 1)
-        nc.sync.dma_start(pos_sb[0][:], pos1)
-        nc.sync.dma_start(pos_sb[1][:], pos2)
-        gate_sb = held([P, 2, T], F32, "gate_sb")
-        nc.sync.dma_start(out=gate_sb[:], in_=gate.rearrange("r p t -> p r t"))
+        def load_list(name):
+            tile, source = {"offs": (offs_sb, offs), "offs2": (offs2_sb, offs2), "pos0": (pos_sb[0], pos1), "pos1": (pos_sb[1], pos2)}[name]
+            nc.sync.dma_start(tile[:], source)
 
-        pairs = {}
-        for s in range(PASSES):
-            for u in range(2):
-                pairs[s, u] = held([P, T, 2], BF16, f"pairs{s}{u}")
-                nc.scalar.copy(out=pairs[s, u][:], in_=xo_raw[s, u][:].rearrange("p j t -> p t j"))
+        def load_gate():
+            nc.sync.dma_start(out=gate_sb[:], in_=gate.rearrange("r p t -> p r t"))
+
+        loaders = {"Llist": load_list, "Lfw": load_far_words, "Lfs": load_far_scales, "Lxo": load_xo, "Lw1": load_w1, "Lw2": load_w2, "Lgate": load_gate}
+        for step in LOADS:
+            loaders[step[0]](*step[1:])
+
+        def cast(engine, target, source):
+            if engine == "scalar":
+                nc.scalar.copy(out=target, in_=source)
+            elif engine == "vector":
+                nc.vector.tensor_copy(out=target, in_=source)
+            else:
+                nc.gpsimd.tensor_scalar(target, source, 1.0, 0.0, MULT, ADD)
+
+        tiles = {}
+
+        def once(shape, dtype, name):
+            if name not in tiles:
+                tiles[name] = held(shape, dtype, name)
+            return tiles[name]
+
+        pairs, picked, own, far_w, far_s, first, second, h_banks, hidden, h_codes, sums = ({} for i in range(11))
+
+        def cast_xo(s, u):
+            w = 2 * s + u
+            target = pair_words[:, w * T : (w + 1) * T].bitcast(BF16).rearrange("p (t j) -> p t j", j=2)
+            cast(XO_ENGINE[2 * s + u], target, xo_raw[s, u][:].rearrange("p j t -> p t j"))
 
         def quantize(values, width, name):
             codes = held([P, width], U32, name + "_codes")
@@ -108,109 +250,125 @@ def tile_moe_loc_mlp_relu_kernel(tc, x_words, x_scales, xo, w1, w2, gate, offs, 
             return codes, scales
 
         def expert_list(tile, e):
-            return tile[:, e * LIST_COLS : (e + 1) * LIST_COLS]
+            return tile[:, 2 * e * LIST_COLS : 2 * (e + 1) * LIST_COLS]
 
-        def own_tokens(e):
-            picked = held([P, 2, PASSES * C], U32, f"picked{e}", slot=PICKED_SLOT[e])
-            for s in range(PASSES):
-                for u in range(2):
-                    window = pairs[s, u][:].rearrange("p t j -> p (t j)").bitcast(U32)
-                    nc.vector.tensor_copy(picked[:, u, s * C : (s + 1) * C], window.indirect(expert_list(offs_sb, e)))
-            grouped = held([P, PASSES * C * PACK], BF16, f"own_grouped{e}")
+        def pick_own(pair, s, u):
+            picked = once([P, 2, 2 * C], U32, f"picked{2 * pair + s}")
+            w = 2 * s + u
+            window = pair_words[:, w * T : (w + 2) * T].bitcast(U32)
+            nc.vector.tensor_copy(picked[:, u, :], window.indirect(expert_list(offs_sb, pair)))
+
+        def group_own(k):
+            grouped = once([P, 2 * C * PACK], BF16, f"own_grouped{k}")
             nc.vector.tensor_copy(
                 out=grouped[:].bitcast(I32).rearrange("p (c u) -> p c u", u=2),
-                in_=picked[:].bitcast(I32).rearrange("p u c -> p c u"),
+                in_=tiles[f"picked{k}"][:].bitcast(I32).rearrange("p u c -> p c u"),
             )
-            codes, scales = quantize(grouped[:], PASSES * C, f"own{e}")
-            return [(codes[:, s * C : (s + 1) * C], scales[:, s * C : (s + 1) * C]) for s in range(PASSES)]
 
-        def far_tokens(e):
-            scales = held([P, D], U8, f"far_picked_scales{e}", slot=FAR_SCALE_SLOT[e])
-            nc.vector.tensor_copy(scales[:], far_scales[:].bitcast(U8).indirect(expert_list(offs2_sb, e)))
-            operands = []
-            for s in range(PASSES):
-                words = held([P, D], U32, f"far_picked_words{e}{s}", slot=FAR_WORD_SLOT[e] if s else None)
-                nc.vector.tensor_copy(words[:], far_words[s][:].bitcast(U32).indirect(expert_list(offs2_sb, e)))
-                operands.append((words[:], scales[4 * s : P, :]))
-            return operands
+        def quantize_own(k):
+            own[k] = quantize(tiles[f"own_grouped{k}"][:], 2 * C, f"own{k}")
 
-        def first_matrix(e):
-            operands = []
-            for s in range(PASSES):
-                grouped = held([P, H * PACK], BF16, f"w1_grouped{e}{s}", slot=f"w1_grouped{e % 2 if s == 0 else e}{s}")
-                nc.scalar.copy(
-                    out=grouped[:].rearrange("p (t m j) -> p m j t", t=PACK, j=PACK),
-                    in_=w1_raw[e, s][:].rearrange("p j (m t) -> p m j t", t=PACK),
-                )
-                operands.append(quantize(grouped[:], H, f"w1_{e}{s}"))
-            return operands
+        def pick_far_words(pair, s):
+            far_w[pair, s] = held([P, 2 * D], U32, f"far_w{pair}{s}")
+            window = far_words[:, s * Q : (s + 2) * Q].bitcast(U32)
+            nc.vector.tensor_copy(far_w[pair, s][:], window.indirect(expert_list(offs2_sb, pair)))
 
-        def second_matrix(e):
-            grouped = held([P, N * PACK], BF16, f"w2_grouped{e}")
-            nc.vector.tensor_copy(
-                out=grouped[:].rearrange("p (c i j) -> p c j i", i=4, j=PACK),
-                in_=w2_raw[e][:].rearrange("p j (c i) -> p c j i", i=4),
+        def pick_far_scales(pair):
+            far_s[pair] = held([P, 2 * D], U8, f"far_s{pair}")
+            nc.vector.tensor_copy(far_s[pair][:], far_scales[:].bitcast(U8).indirect(expert_list(offs2_sb, pair)))
+
+        def cast_w1(e, s, a):
+            grouped = once([P, H * PACK], BF16, f"w1_grouped{e}{s}")
+            target = grouped[:].rearrange("p (a b c i j) -> p a c j i b", a=2, b=2, i=2, j=PACK)
+            source = w1_raw[e, s][:].rearrange("p j (c a i b) -> p a c j i b", a=2, i=2, b=2)
+            engine = W1_ENGINE.get((e, s, a), "scalar")
+            if engine == "gpsimd":
+                for b in range(2):
+                    cast(engine, target[:, a, :, :, :, b], source[:, a, :, :, :, b])
+            else:
+                cast(engine, target[:, a], source[:, a])
+
+        def quantize_w1(e, s):
+            first[e, s] = quantize(tiles[f"w1_grouped{e}{s}"][:], H, f"w1_{e}{s}")
+
+        def cast_w2(e):
+            grouped = once([P, N * PACK], BF16, f"w2_grouped{e}")
+            cast(
+                W2_ENGINE[e],
+                grouped[:].rearrange("p (c i j) -> p c j i", i=4, j=PACK),
+                w2_raw[e][:].rearrange("p j (c i) -> p c j i", i=4),
             )
-            return quantize(grouped[:], N, f"w2_{e}")
 
-        def expert(tokens, first, second, kind, e, h_bufs, y_bufs):
-            hidden = held([P, C, PACK], BF16, f"hidden_{kind}", 2)
-            for half in range(C // P):
-                slots = slice(half * P, (half + 1) * P)
-                bank = psum.tile([P, PACK, P], F32, name=f"h_{kind}", bufs=h_bufs)
-                for t in range(PACK):
-                    cols = slice(t * P, (t + 1) * P)
-                    for s in range(PASSES):
-                        nc.tensor.matmul_mx(
-                            out=bank[:, t, :],
-                            lhsT=first[s][0][:, cols].bitcast(FP8X4),
-                            lhsT_scale=first[s][1][:, cols],
-                            rhs=tokens[s][0][:, slots].bitcast(FP8X4),
-                            rhs_scale=tokens[s][1][:, slots],
-                            start=(s == 0),
-                            stop=(s == PASSES - 1),
-                        )
-                nc.scalar.activation(
-                    out=hidden[:, slots, :], in_=bank[:].rearrange("p t c -> p c t"), func=RELU, bias=no_bias[:]
-                )
-            codes, scales = quantize(hidden[:].rearrange("p c t -> p (c t)"), C, f"h_{kind}{e}")
-            sums = psum.tile([P, N_TILES, C], F32, name=f"y_{kind}", bufs=y_bufs)
+        def quantize_w2(e):
+            second[e] = quantize(tiles[f"w2_grouped{e}"][:], N, f"w2_{e}")
+
+        def first_layer(kind, e, half):
+            if kind == "own":
+                tokens = [own[e // 2 * 2 + s] for s in range(PASSES)]
+            else:
+                tokens = [(far_w[e // 2, s][:], far_s[e // 2][4 * s : P, :]) for s in range(PASSES)]
+            hidden = once([P, C, PACK], BF16, f"hidden_{kind}{e}")
+            slots = slice(half * P, (half + 1) * P)
+            in_pair = slice((e % 2) * C + half * P, (e % 2) * C + (half + 1) * P)
+            bank = psum.tile([P, PACK, P], F32, name=f"h_{kind}", bufs=2 if kind == "own" else 3)
+            for t in range(PACK):
+                cols = slice(t * P, (t + 1) * P)
+                for s in range(PASSES):
+                    nc.tensor.matmul_mx(
+                        out=bank[:, t, :],
+                        lhsT=first[e, s][0][:, cols].bitcast(FP8X4),
+                        lhsT_scale=first[e, s][1][:, cols],
+                        rhs=tokens[s][0][:, in_pair].bitcast(FP8X4),
+                        rhs_scale=tokens[s][1][:, in_pair],
+                        start=(s == 0),
+                        stop=(s == PASSES - 1),
+                    )
+            nc.scalar.activation(
+                out=hidden[:, slots, :], in_=bank[:].rearrange("p t c -> p c t"), func=RELU, bias=no_bias[:]
+            )
+
+        def quantize_hidden(kind, e):
+            hidden = tiles[f"hidden_{kind}{e}"]
+            h_codes[kind, e] = quantize(hidden[:].rearrange("p c t -> p (c t)"), C, f"h_{kind}{e}")
+
+        out_rows = out.rearrange("(nt p) c -> p nt c", p=P)
+        slot_rows = [held([P, E * C], F32, f"slot_rows{nt}") for nt in range(N_TILES)]
+
+        def second_layer(kind, e):
+            codes, scales = h_codes[kind, e]
+            bank = psum.tile([P, N_TILES, C], F32, name=f"y_{kind}", bufs=2 if kind == "own" else 1)
             for nt in range(N_TILES):
                 cols = slice(nt * P, (nt + 1) * P)
                 nc.tensor.matmul_mx(
-                    out=sums[:, nt, :],
-                    lhsT=second[0][:, cols].bitcast(FP8X4),
-                    lhsT_scale=second[1][:, cols],
+                    out=bank[:, nt, :],
+                    lhsT=second[e][0][:, cols].bitcast(FP8X4),
+                    lhsT_scale=second[e][1][:, cols],
                     rhs=codes[:].bitcast(FP8X4),
                     rhs_scale=scales[:],
                     start=True,
                     stop=True,
                 )
-            return sums
+            if kind == "own":
+                for nt in range(N_TILES):
+                    nc.scalar.copy(out=slot_rows[nt][:, e * C : (e + 1) * C], in_=bank[:, nt, :])
+            else:
+                result = held([P, N_TILES, D], F32, f"far_result{e}")
+                cast("vector" if e in Z_ON_VECTOR else "scalar", result[:], bank[:])
+                nc.sync.dma_start(out=out_rows[:, :, T + e * D : T + (e + 1) * D], in_=result[:])
 
-        out_rows = out.rearrange("(nt p) c -> p nt c", p=P)
-        slot_rows = [held([P, E * C], F32, f"slot_rows{nt}") for nt in range(N_TILES)]
-        firsts, seconds = [], []
-        for e in range(E):
-            tokens = own_tokens(e)
-            firsts.append(first_matrix(e))
-            seconds.append(second_matrix(e))
-            sums = expert(tokens, firsts[e], seconds[e], "own", e, 3, 2)
-            for nt in range(N_TILES):
-                nc.scalar.copy(out=slot_rows[nt][:, e * C : (e + 1) * C], in_=sums[:, nt, :])
+        parts = {}
 
-        for e in range(E):
-            sums = expert(far_tokens(e), firsts[e], seconds[e], "far", e, 2, 1)
-            result = held([P, N_TILES, D], F32, f"far_result{e}", slot=f"w1_raw{1 + e // 2}{e % 2}")
-            nc.scalar.copy(out=result[:], in_=sums[:])
-            nc.sync.dma_start(out=out_rows[:, :, T + e * D : T + (e + 1) * D], in_=result[:])
+        def weighted(nt, r):
+            parts[nt, r] = held([P, T], F32, f"part{nt}{r}")
+            nc.vector.tensor_tensor(parts[nt, r][:], slot_rows[nt][:].indirect(pos_sb[r][:]), gate_sb[:, r, :], MULT)
 
-        for nt in range(N_TILES):
-            parts = []
-            for r in range(2):
-                part = held([P, T], F32, f"part{nt}{r}", slot=f"xo_raw{nt}{r}")
-                nc.vector.tensor_tensor(part[:], slot_rows[nt][:].indirect(pos_sb[r][:]), gate_sb[:, r, :], MULT)
-                parts.append(part)
-            combined = held([P, T], F32, f"combined{nt}", slot=f"w1_raw0{nt}")
-            nc.vector.tensor_tensor(combined[:], parts[0][:], parts[1][:], ADD)
+        def combine(nt):
+            combined = held([P, T], F32, f"combined{nt}")
+            nc.vector.tensor_tensor(combined[:], parts[nt, 0][:], parts[nt, 1][:], ADD)
             nc.sync.dma_start(out=out_rows[:, nt, 0:T], in_=combined[:])
+
+        steps = {"cx": cast_xo, "og": pick_own, "il": group_own, "qo": quantize_own, "fw": pick_far_words, "fs": pick_far_scales,
+                 "c1": cast_w1, "q1": quantize_w1, "c2": cast_w2, "q2": quantize_w2, "h": first_layer, "qh": quantize_hidden,
+                 "y": second_layer, "cg": weighted, "add": combine}
+        for step in ORDER:
+            steps[step[0]](*step[1:])

@@ -30,127 +30,129 @@ SLOT = {
     "part11": "xo_raw11",
     "combined0": "picked0",
     "combined1": "picked1",
-    "far_s1": "w1_raw11",
-    "hidden_own2": "w1_raw31",
+    "hidden_own0": "w1_raw20",
+    "hidden_far0": "w1_grouped21",
+    "w2_grouped0": "w1_grouped01",
     "far_result2": "w1_raw11",
-    "far_result3": "w1_raw21",
-    "hidden_own0": "w1_grouped11",
-    "hidden_own1": "w2_grouped0",
-    "hidden_far1": "w2_raw1",
-    "far_result0": "w1_raw00",
-    "w1_grouped31": "w1_raw11",
-    "own_grouped2": "w1_raw20",
-    "hidden_own3": "w2_grouped0",
-    "hidden_far2": "w1_raw20",
-    "w2_grouped1": "w1_raw00",
-    "own_grouped0": "w1_grouped21",
-    "own_grouped3": "xo_raw11",
-    "hidden_far3": "xo_raw11",
-    "w1_grouped30": "xo_raw10",
-    "far_result1": "own_grouped1",
+    "far_result3": "w1_raw20",
+    "own_grouped3": "w1_raw21",
+    "hidden_own1": "w1_raw30",
+    "far_w10": "w1_raw31",
+    "picked3": "w1_grouped01",
+    "hidden_far2": "w2_raw3",
+    "own_grouped2": "xo_raw01",
+    "far_result1": "w1_raw20",
+    "own_grouped1": "xo_raw10",
+    "hidden_far3": "w1_raw30",
+    "far_s1": "w1_grouped00",
+    "hidden_far1": "own_grouped0",
+    "far_result0": "xo_raw10",
+    "w2_grouped2": "w1_raw11",
+    "w1_grouped30": "w1_raw11",
+    "hidden_own2": "w1_grouped01",
 }
 
-LOADS = [("Lfw", 1), ("Llist", "offs2"), ("Lxo", 1, 1), ("Lxo", 1, 0), ("Llist", "offs"), ("Lxo", 0, 1), ("Lxo", 0, 0), ("Lw1", 0, 0), ("Lw1", 0, 1), ("Lw1", 1, 0), ("Llist", "pos1"), ("Lw1", 1, 1), ("Lw1", 2, 0), ("Lfw", 0), ("Lfs",), ("Lw1", 2, 1), ("Lw2", 0), ("Lw1", 3, 0), ("Lgate",), ("Llist", "pos0"), ("Lw1", 3, 1), ("Lw2", 1), ("Lw2", 2), ("Lw2", 3)]
+LOADS = [("Lfw", 1), ("Llist", "offs2"), ("Lxo", 1, 1), ("Lxo", 1, 0), ("Llist", "offs"), ("Lfw", 0), ("Lxo", 0, 1), ("Lw1", 0, 0), ("Lxo", 0, 0), ("Lw1", 0, 1), ("Lw1", 1, 0), ("Lfs",), ("Lw1", 1, 1), ("Lw1", 2, 0), ("Lw2", 0), ("Lw1", 2, 1), ("Lw1", 3, 0), ("Lw1", 3, 1), ("Lw2", 1), ("Lw2", 2), ("Lw2", 3), ("Llist", "pos1"), ("Llist", "pos0"), ("Lgate",)]
 ORDER = [
-    ("fw", 0, 1),
-    ("fw", 0, 0),
-    ("c1", 0, 0, 0),
-    ("c2", 0),
-    ("c1", 0, 0, 1),
-    ("c1", 0, 1, 0),
     ("cx", 1, 1),
     ("og", 0, 1, 1),
-    ("c2", 1),
-    ("q1", 0, 0),
+    ("c1", 0, 0, 0),
+    ("c1", 0, 0, 1),
     ("cx", 1, 0),
-    ("c1", 0, 1, 1),
-    ("cx", 0, 1),
+    ("c1", 0, 1, 0),
     ("og", 0, 1, 0),
-    ("il", 1),
-    ("q2", 0),
-    ("qo", 1),
-    ("q2", 1),
-    ("cx", 0, 0),
-    ("c2", 2),
+    ("cx", 0, 1),
     ("og", 0, 0, 1),
+    ("cx", 0, 0),
+    ("c1", 0, 1, 1),
+    ("fw", 0, 1),
+    ("q1", 0, 0),
+    ("fs", 0),
     ("og", 0, 0, 0),
-    ("q2", 2),
-    ("og", 1, 1, 1),
-    ("q1", 0, 1),
-    ("og", 1, 1, 0),
     ("c1", 1, 0, 0),
-    ("il", 0),
+    ("q1", 0, 1),
+    ("il", 1),
     ("c1", 1, 0, 1),
-    ("c2", 3),
-    ("il", 3),
     ("c1", 1, 1, 0),
-    ("c1", 1, 1, 1),
+    ("il", 0),
+    ("fw", 0, 0),
     ("q1", 1, 0),
+    ("c1", 1, 1, 1),
     ("c1", 2, 0, 0),
     ("c1", 2, 0, 1),
-    ("qo", 0),
-    ("q1", 1, 1),
-    ("og", 1, 0, 1),
+    ("qo", 1),
     ("c1", 2, 1, 0),
-    ("q1", 2, 0),
     ("c1", 2, 1, 1),
-    ("h", "own", 0, 0),
-    ("h", "own", 0, 1),
-    ("og", 1, 0, 0),
+    ("og", 1, 1, 1),
     ("c1", 3, 0, 0),
-    ("il", 2),
-    ("fs", 0),
-    ("h", "own", 1, 0),
-    ("qo", 3),
-    ("qh", "own", 0),
-    ("c1", 3, 0, 1),
+    ("og", 1, 1, 0),
+    ("q1", 1, 1),
+    ("il", 3),
+    ("og", 1, 0, 1),
+    ("qo", 0),
+    ("og", 1, 0, 0),
+    ("h", "own", 0, 0),
+    ("q1", 2, 0),
     ("q1", 2, 1),
-    ("h", "own", 1, 1),
-    ("qh", "own", 1),
+    ("c2", 0),
+    ("c1", 3, 0, 1),
+    ("qo", 3),
     ("h", "far", 0, 0),
-    ("c1", 3, 1, 0),
-    ("h", "far", 0, 1),
-    ("qh", "far", 0),
     ("q1", 3, 0),
-    ("c1", 3, 1, 1),
-    ("y", "own", 0),
+    ("h", "own", 0, 1),
+    ("il", 2),
+    ("c2", 1),
     ("qo", 2),
-    ("h", "own", 2, 0),
-    ("q1", 3, 1),
-    ("h", "own", 2, 1),
+    ("qh", "own", 0),
+    ("q2", 0),
+    ("h", "own", 1, 0),
+    ("c1", 3, 1, 0),
+    ("h", "own", 1, 1),
+    ("h", "far", 0, 1),
+    ("c2", 2),
+    ("c1", 3, 1, 1),
     ("fw", 1, 1),
+    ("h", "own", 2, 0),
+    ("q2", 1),
+    ("qh", "far", 0),
+    ("c2", 3),
     ("h", "far", 1, 0),
+    ("h", "own", 2, 1),
+    ("q1", 3, 1),
+    ("qh", "own", 1),
     ("h", "own", 3, 0),
-    ("h", "own", 3, 1),
-    ("fs", 1),
-    ("fw", 1, 0),
-    ("q2", 3),
     ("h", "far", 1, 1),
-    ("h", "far", 2, 0),
+    ("fw", 1, 0),
     ("qh", "own", 2),
+    ("fs", 1),
+    ("h", "own", 3, 1),
+    ("q2", 2),
+    ("q2", 3),
+    ("y", "own", 0),
     ("y", "own", 1),
+    ("h", "far", 2, 0),
     ("qh", "own", 3),
     ("y", "far", 0),
-    ("y", "own", 2),
     ("h", "far", 2, 1),
+    ("qh", "far", 1),
+    ("y", "own", 2),
     ("y", "own", 3),
+    ("cg", 0, 0),
+    ("qh", "far", 2),
+    ("cg", 1, 1),
+    ("y", "far", 1),
     ("h", "far", 3, 0),
     ("h", "far", 3, 1),
-    ("qh", "far", 1),
-    ("y", "far", 1),
-    ("qh", "far", 2),
-    ("cg", 1, 0),
-    ("cg", 0, 1),
     ("qh", "far", 3),
-    ("cg", 1, 1),
+    ("cg", 0, 1),
+    ("cg", 1, 0),
     ("y", "far", 2),
-    ("add", 1),
-    ("cg", 0, 0),
-    ("y", "far", 3),
     ("add", 0),
+    ("y", "far", 3),
+    ("add", 1),
 ]
-W1_ENGINE = {(3, 0, 0): "vector", (3, 0, 1): "vector", (3, 1, 0): "vector"}
-W2_ENGINE = ["scalar", "vector", "vector", "vector"]
+W1_ENGINE = {(3, 1, 0): "vector", (3, 1, 1): "vector"}
+W2_ENGINE = ["vector", "scalar", "vector", "vector"]
 XO_ENGINE = ["scalar", "scalar", "scalar", "scalar"]
 Z_ON_VECTOR = [0]
 
@@ -310,7 +312,7 @@ def tile_moe_loc_mlp_relu_kernel(tc, x_words, x_scales, xo, w1, w2, gate, offs, 
             hidden = once([P, C, PACK], BF16, f"hidden_{kind}{e}")
             slots = slice(half * P, (half + 1) * P)
             in_pair = slice((e % 2) * C + half * P, (e % 2) * C + (half + 1) * P)
-            bank = psum.tile([P, PACK, P], F32, name=f"h_{kind}", bufs=2 if kind == "own" else 3)
+            bank = psum.tile([P, PACK, P], F32, name=f"h_{kind}", bufs=3 if kind == "own" else 2)
             for t in range(PACK):
                 cols = slice(t * P, (t + 1) * P)
                 for s in range(PASSES):

@@ -30,130 +30,130 @@ SLOT = {
     "part11": "xo_raw11",
     "combined0": "picked0",
     "combined1": "picked1",
-    "hidden_own0": "w1_raw20",
-    "hidden_far0": "w1_grouped21",
-    "w2_grouped0": "w1_grouped01",
+    "hidden_far0": "w1_raw01",
     "far_result2": "w1_raw11",
     "far_result3": "w1_raw20",
     "own_grouped3": "w1_raw21",
-    "hidden_own1": "w1_raw30",
-    "far_w10": "w1_raw31",
-    "picked3": "w1_grouped01",
-    "hidden_far2": "w2_raw3",
-    "own_grouped2": "xo_raw01",
-    "far_result1": "w1_raw20",
-    "own_grouped1": "xo_raw10",
-    "hidden_far3": "w1_raw30",
-    "far_s1": "w1_grouped00",
-    "hidden_far1": "own_grouped0",
-    "far_result0": "xo_raw10",
-    "w2_grouped2": "w1_raw11",
-    "w1_grouped30": "w1_raw11",
-    "hidden_own2": "w1_grouped01",
+    "hidden_own1": "w1_grouped21",
+    "far_w10": "w2_raw0",
+    "picked3": "w1_raw01",
+    "far_w00": "w1_raw10",
+    "hidden_far3": "w2_raw2",
+    "w1_grouped31": "w1_raw30",
+    "w2_grouped2": "xo_raw00",
+    "w2_grouped3": "w1_grouped10",
+    "hidden_far1": "w1_raw11",
+    "hidden_own3": "w1_grouped01",
+    "own_grouped0": "xo_raw01",
+    "hidden_own2": "picked2",
+    "w2_grouped1": "xo_raw01",
+    "own_grouped2": "xo_raw00",
+    "far_result0": "w1_grouped21",
 }
 
-LOADS = [("Lfw", 1), ("Llist", "offs2"), ("Lxo", 1, 1), ("Lxo", 1, 0), ("Llist", "offs"), ("Lfw", 0), ("Lxo", 0, 1), ("Lw1", 0, 0), ("Lxo", 0, 0), ("Lw1", 0, 1), ("Lw1", 1, 0), ("Lfs",), ("Lw1", 1, 1), ("Lw1", 2, 0), ("Lw2", 0), ("Lw1", 2, 1), ("Lw1", 3, 0), ("Lw1", 3, 1), ("Lw2", 1), ("Lw2", 2), ("Lw2", 3), ("Llist", "pos1"), ("Llist", "pos0"), ("Lgate",)]
+LOADS = [("Lfw", 1), ("Llist", "offs"), ("Llist", "offs2"), ("Lxo", 1, 1), ("Lxo", 1, 0), ("Lxo", 0, 1), ("Lxo", 0, 0), ("Lw1", 0, 0), ("Lfw", 0), ("Lw1", 0, 1), ("Lw1", 1, 0), ("Lw1", 1, 1), ("Lw1", 2, 0), ("Lfs",), ("Lw1", 2, 1), ("Lw1", 3, 0), ("Lw2", 0), ("Lw1", 3, 1), ("Lw2", 1), ("Lw2", 2), ("Lw2", 3), ("Llist", "pos1"), ("Llist", "pos0"), ("Lgate",)]
 ORDER = [
     ("cx", 1, 1),
-    ("og", 0, 1, 1),
     ("c1", 0, 0, 0),
     ("c1", 0, 0, 1),
-    ("cx", 1, 0),
     ("c1", 0, 1, 0),
-    ("og", 0, 1, 0),
-    ("cx", 0, 1),
-    ("og", 0, 0, 1),
-    ("cx", 0, 0),
     ("c1", 0, 1, 1),
-    ("fw", 0, 1),
+    ("og", 0, 1, 1),
+    ("cx", 1, 0),
+    ("cx", 0, 1),
     ("q1", 0, 0),
-    ("fs", 0),
-    ("og", 0, 0, 0),
+    ("cx", 0, 0),
     ("c1", 1, 0, 0),
-    ("q1", 0, 1),
-    ("il", 1),
     ("c1", 1, 0, 1),
     ("c1", 1, 1, 0),
-    ("il", 0),
-    ("fw", 0, 0),
-    ("q1", 1, 0),
+    ("q1", 0, 1),
+    ("og", 0, 1, 0),
+    ("og", 0, 0, 1),
     ("c1", 1, 1, 1),
+    ("il", 1),
+    ("og", 0, 0, 0),
     ("c1", 2, 0, 0),
+    ("q1", 1, 0),
     ("c1", 2, 0, 1),
-    ("qo", 1),
     ("c1", 2, 1, 0),
-    ("c1", 2, 1, 1),
+    ("il", 0),
+    ("c2", 0),
     ("og", 1, 1, 1),
-    ("c1", 3, 0, 0),
-    ("og", 1, 1, 0),
+    ("fw", 0, 1),
     ("q1", 1, 1),
-    ("il", 3),
-    ("og", 1, 0, 1),
+    ("qo", 1),
+    ("og", 1, 1, 0),
+    ("q2", 0),
     ("qo", 0),
-    ("og", 1, 0, 0),
+    ("og", 1, 0, 1),
+    ("c1", 2, 1, 1),
+    ("c2", 1),
     ("h", "own", 0, 0),
     ("q1", 2, 0),
+    ("il", 3),
+    ("fw", 0, 0),
     ("q1", 2, 1),
-    ("c2", 0),
-    ("c1", 3, 0, 1),
-    ("qo", 3),
-    ("h", "far", 0, 0),
-    ("q1", 3, 0),
+    ("c1", 3, 0, 0),
+    ("fs", 0),
     ("h", "own", 0, 1),
-    ("il", 2),
-    ("c2", 1),
-    ("qo", 2),
-    ("qh", "own", 0),
-    ("q2", 0),
-    ("h", "own", 1, 0),
-    ("c1", 3, 1, 0),
-    ("h", "own", 1, 1),
+    ("c1", 3, 0, 1),
+    ("h", "far", 0, 0),
     ("h", "far", 0, 1),
-    ("c2", 2),
-    ("c1", 3, 1, 1),
-    ("fw", 1, 1),
-    ("h", "own", 2, 0),
     ("q2", 1),
-    ("qh", "far", 0),
-    ("c2", 3),
-    ("h", "far", 1, 0),
-    ("h", "own", 2, 1),
-    ("q1", 3, 1),
-    ("qh", "own", 1),
-    ("h", "own", 3, 0),
-    ("h", "far", 1, 1),
+    ("fw", 1, 1),
+    ("h", "own", 1, 0),
+    ("h", "own", 1, 1),
+    ("q1", 3, 0),
+    ("c1", 3, 1, 0),
     ("fw", 1, 0),
-    ("qh", "own", 2),
     ("fs", 1),
-    ("h", "own", 3, 1),
-    ("q2", 2),
-    ("q2", 3),
+    ("og", 1, 0, 0),
+    ("qh", "own", 0),
+    ("c1", 3, 1, 1),
+    ("qo", 3),
+    ("il", 2),
     ("y", "own", 0),
-    ("y", "own", 1),
+    ("qo", 2),
+    ("q1", 3, 1),
+    ("c2", 2),
+    ("h", "far", 1, 0),
+    ("h", "far", 1, 1),
+    ("qh", "own", 1),
+    ("h", "own", 2, 0),
+    ("h", "own", 2, 1),
     ("h", "far", 2, 0),
-    ("qh", "own", 3),
-    ("y", "far", 0),
     ("h", "far", 2, 1),
-    ("qh", "far", 1),
-    ("y", "own", 2),
-    ("y", "own", 3),
-    ("cg", 0, 0),
-    ("qh", "far", 2),
-    ("cg", 1, 1),
-    ("y", "far", 1),
+    ("h", "own", 3, 0),
+    ("h", "own", 3, 1),
+    ("y", "own", 1),
     ("h", "far", 3, 0),
     ("h", "far", 3, 1),
+    ("qh", "own", 2),
+    ("q2", 2),
+    ("qh", "far", 0),
+    ("qh", "own", 3),
+    ("c2", 3),
+    ("qh", "far", 1),
+    ("q2", 3),
+    ("qh", "far", 2),
+    ("y", "far", 0),
+    ("y", "own", 2),
     ("qh", "far", 3),
+    ("y", "own", 3),
+    ("cg", 0, 0),
+    ("y", "far", 1),
+    ("cg", 1, 1),
     ("cg", 0, 1),
     ("cg", 1, 0),
+    ("add", 1),
     ("y", "far", 2),
     ("add", 0),
     ("y", "far", 3),
-    ("add", 1),
 ]
-W1_ENGINE = {(3, 1, 0): "vector", (3, 1, 1): "vector"}
-W2_ENGINE = ["vector", "scalar", "vector", "vector"]
+W1_ENGINE = {(1, 1, 0): "vector", (1, 1, 1): "vector", (3, 1, 0): "vector", (3, 1, 1): "vector"}
+W2_ENGINE = ["scalar", "vector", "vector", "vector"]
 XO_ENGINE = ["scalar", "scalar", "scalar", "scalar"]
+GROUP_ON_SCALAR = [1]
 Z_ON_VECTOR = [0]
 
 
@@ -262,10 +262,16 @@ def tile_moe_loc_mlp_relu_kernel(tc, x_words, x_scales, xo, w1, w2, gate, offs, 
 
         def group_own(k):
             grouped = once([P, 2 * C * PACK], BF16, f"own_grouped{k}")
-            nc.vector.tensor_copy(
-                out=grouped[:].bitcast(I32).rearrange("p (c u) -> p c u", u=2),
-                in_=tiles[f"picked{k}"][:].bitcast(I32).rearrange("p u c -> p c u"),
-            )
+            if k in GROUP_ON_SCALAR:
+                nc.scalar.copy(
+                    out=grouped[:].bitcast(F32).rearrange("p (c u) -> p c u", u=2),
+                    in_=tiles[f"picked{k}"][:].bitcast(F32).rearrange("p u c -> p c u"),
+                )
+            else:
+                nc.vector.tensor_copy(
+                    out=grouped[:].bitcast(I32).rearrange("p (c u) -> p c u", u=2),
+                    in_=tiles[f"picked{k}"][:].bitcast(I32).rearrange("p u c -> p c u"),
+                )
 
         def quantize_own(k):
             own[k] = quantize(tiles[f"own_grouped{k}"][:], 2 * C, f"own{k}")
@@ -312,7 +318,7 @@ def tile_moe_loc_mlp_relu_kernel(tc, x_words, x_scales, xo, w1, w2, gate, offs, 
             hidden = once([P, C, PACK], BF16, f"hidden_{kind}{e}")
             slots = slice(half * P, (half + 1) * P)
             in_pair = slice((e % 2) * C + half * P, (e % 2) * C + (half + 1) * P)
-            bank = psum.tile([P, PACK, P], F32, name=f"h_{kind}", bufs=3 if kind == "own" else 2)
+            bank = psum.tile([P, PACK, P], F32, name=f"h_{kind}", bufs=2 if kind == "own" else 2)
             for t in range(PACK):
                 cols = slice(t * P, (t + 1) * P)
                 for s in range(PASSES):
@@ -338,7 +344,7 @@ def tile_moe_loc_mlp_relu_kernel(tc, x_words, x_scales, xo, w1, w2, gate, offs, 
 
         def second_layer(kind, e):
             codes, scales = h_codes[kind, e]
-            bank = psum.tile([P, N_TILES, C], F32, name=f"y_{kind}", bufs=2 if kind == "own" else 1)
+            bank = psum.tile([P, N_TILES, C], F32, name=f"y_{kind}", bufs=2 if kind == "own" else 2)
             for nt in range(N_TILES):
                 cols = slice(nt * P, (nt + 1) * P)
                 nc.tensor.matmul_mx(

from contextlib import ExitStack

import concourse.mybir as mybir

K, T, Q, E, C, D, H, N = 1024, 512, 512, 4, 256, 256, 512, 256
FLOPS = 2 * E * (C + D) * (K * H + H * N)

F32 = mybir.dt.float32
BF16 = mybir.dt.bfloat16
I32 = mybir.dt.int32
U32 = mybir.dt.uint32
U16 = mybir.dt.uint16
U8 = mybir.dt.uint8
FP8X4 = mybir.dt.float8_e4m3fn_x4
RELU = mybir.ActivationFunctionType.Relu
MULT = mybir.AluOpType.mult
ADD = mybir.AluOpType.add

P = 128
PACK = 4
K_PASS = P * PACK
PASSES = K // K_PASS
LIST_COLS = C // 16
N_TILES = N // P

SLOT = {
    "part00": "xo_raw00",
    "part01": "xo_raw01",
    "part10": "xo_raw10",
    "part11": "xo_raw11",
    "combined0": "picked0",
    "combined1": "picked1",
    "hidden_far0": "w1_raw01",
    "far_result2": "w1_raw11",
    "far_result3": "w1_raw20",
    "own_grouped3": "w1_raw21",
    "hidden_own1": "w1_grouped21",
    "far_w10": "w2_raw0",
    "picked3": "w1_raw01",
    "far_w00": "w1_raw10",
    "hidden_far3": "w2_raw2",
    "w1_grouped31": "w1_raw30",
    "w2_grouped2": "xo_raw00",
    "w2_grouped3": "w1_grouped10",
    "hidden_far1": "w1_raw11",
    "hidden_own3": "w1_grouped01",
    "own_grouped0": "xo_raw01",
    "hidden_own2": "picked2",
    "w2_grouped1": "xo_raw01",
    "own_grouped2": "xo_raw00",
    "far_result0": "w1_grouped21",
}

LOADS = [("Lfw", 1), ("Llist", "offs"), ("Llist", "offs2"), ("Lxo", 1, 1), ("Lxo", 1, 0), ("Lxo", 0, 1), ("Lxo", 0, 0), ("Lw1", 0, 0), ("Lfw", 0), ("Lw1", 0, 1), ("Lw1", 1, 0), ("Lw1", 1, 1), ("Lw1", 2, 0), ("Lfs",), ("Lw1", 2, 1), ("Lw1", 3, 0), ("Lw2", 0), ("Lw1", 3, 1), ("Lw2", 1), ("Lw2", 2), ("Lw2", 3), ("Llist", "pos1"), ("Llist", "pos0"), ("Lgate",)]
ORDER = [
    ("cx", 1, 1),
    ("c1", 0, 0, 0),
    ("c1", 0, 0, 1),
    ("c1", 0, 1, 0),
    ("c1", 0, 1, 1),
    ("og", 0, 1, 1),
    ("cx", 1, 0),
    ("cx", 0, 1),
    ("q1", 0, 0),
    ("cx", 0, 0),
    ("c1", 1, 0, 0),
    ("c1", 1, 0, 1),
    ("c1", 1, 1, 0),
    ("q1", 0, 1),
    ("og", 0, 1, 0),
    ("og", 0, 0, 1),
    ("c1", 1, 1, 1),
    ("il", 1),
    ("og", 0, 0, 0),
    ("c1", 2, 0, 0),
    ("q1", 1, 0),
    ("c1", 2, 0, 1),
    ("c1", 2, 1, 0),
    ("il", 0),
    ("c2", 0),
    ("og", 1, 1, 1),
    ("fw", 0, 1),
    ("q1", 1, 1),
    ("qo", 1),
    ("og", 1, 1, 0),
    ("q2", 0),
    ("qo", 0),
    ("og", 1, 0, 1),
    ("c1", 2, 1, 1),
    ("c2", 1),
    ("h", "own", 0, 0),
    ("q1", 2, 0),
    ("il", 3),
    ("fw", 0, 0),
    ("q1", 2, 1),
    ("c1", 3, 0, 0),
    ("fs", 0),
    ("h", "own", 0, 1),
    ("c1", 3, 0, 1),
    ("h", "far", 0, 0),
    ("h", "far", 0, 1),
    ("q2", 1),
    ("fw", 1, 1),
    ("h", "own", 1, 0),
    ("h", "own", 1, 1),
    ("q1", 3, 0),
    ("c1", 3, 1, 0),
    ("fw", 1, 0),
    ("fs", 1),
    ("og", 1, 0, 0),
    ("qh", "own", 0),
    ("c1", 3, 1, 1),
    ("qo", 3),
    ("il", 2),
    ("y", "own", 0),
    ("qo", 2),
    ("q1", 3, 1),
    ("c2", 2),
    ("h", "far", 1, 0),
    ("h", "far", 1, 1),
    ("qh", "own", 1),
    ("h", "own", 2, 0),
    ("h", "own", 2, 1),
    ("h", "far", 2, 0),
    ("h", "far", 2, 1),
    ("h", "own", 3, 0),
    ("h", "own", 3, 1),
    ("y", "own", 1),
    ("h", "far", 3, 0),
    ("h", "far", 3, 1),
    ("qh", "own", 2),
    ("q2", 2),
    ("qh", "far", 0),
    ("qh", "own", 3),
    ("c2", 3),
    ("qh", "far", 1),
    ("q2", 3),
    ("qh", "far", 2),
    ("y", "far", 0),
    ("y", "own", 2),
    ("qh", "far", 3),
    ("y", "own", 3),
    ("cg", 0, 0),
    ("y", "far", 1),
    ("cg", 1, 1),
    ("cg", 0, 1),
    ("cg", 1, 0),
    ("add", 1),
    ("y", "far", 2),
    ("add", 0),
    ("y", "far", 3),
]
W1_ENGINE = {(1, 1, 0): "vector", (1, 1, 1): "vector", (3, 1, 0): "vector", (3, 1, 1): "vector"}
W2_ENGINE = ["scalar", "vector", "vector", "vector"]
XO_ENGINE = ["scalar", "scalar", "scalar", "scalar"]
GROUP_ON_SCALAR = [1]
Z_ON_VECTOR = [0]


def tile_moe_loc_mlp_relu_kernel(tc, x_words, x_scales, xo, w1, w2, gate, offs, pos1, pos2, offs2, out):
    nc = tc.nc
    with ExitStack() as ctx:
        lists = ctx.enter_context(tc.tile_pool(name="lists", bufs=1))
        keep = ctx.enter_context(tc.tile_pool(name="keep", bufs=1))
        psum = ctx.enter_context(tc.psum_pool(name="psum", bufs=1))

        def held(shape, dtype, name):
            return keep.tile(shape, dtype, name=name, tag=SLOT.get(name, name), align_bytes=64)

        offs_sb = lists.tile([P, E * LIST_COLS], U16, name="offs_sb")
        offs2_sb = lists.tile([P, E * LIST_COLS], U16, name="offs2_sb")
        pos_sb = [lists.tile([P, T // 16], U16, name=f"pos_sb{r}") for r in range(2)]

        zero = held([P, 1], F32, "zero")
        no_bias = held([P, 1], F32, "no_bias")
        nc.vector.memset(zero[:], 0.0)
        nc.scalar.activation(out=no_bias[:], in_=zero[:], func=RELU)

        far_scales = held([P, 2 * Q // 4], I32, "far_scales")
        nc.vector.memset(far_scales[:], 0)

        far_words = held([P, (PASSES + 1) * Q], I32, "far_words")
        nc.vector.memset(far_words[:, PASSES * Q :], 0)
        pair_words = held([P, (2 * PASSES + 1) * T], I32, "pair_words")
        nc.vector.memset(pair_words[:, 2 * PASSES * T :], 0)
        gate_sb = held([P, 2, T], F32, "gate_sb")
        xo_raw, w1_raw, w2_raw = {}, {}, {}

        def load_far_words(s):
            nc.sync.dma_start(out=far_words[:, s * Q : (s + 1) * Q], in_=x_words[s].rearrange("p t d -> p (t d)").bitcast(I32))

        def load_far_scales():
            for quad in range(4):
                nc.sync.dma_start(
                    out=far_scales[32 * quad : 32 * quad + 4 * PASSES, 0 : Q // 4],
                    in_=x_scales[:, 4 * quad : 4 * quad + 4, :].bitcast(I32),
                )

        def load_xo(s, u):
            xo_raw[s, u] = held([P, 2, T], F32, f"xo_raw{s}{u}")
            rows = xo[s * K_PASS : (s + 1) * K_PASS, :].rearrange("(p j) t -> p j t", j=PACK)
            nc.sync.dma_start(out=xo_raw[s, u][:], in_=rows[:, 2 * u : 2 * u + 2, :])

        def load_w1(e, s):
            w1_raw[e, s] = held([P, PACK, H], F32, f"w1_raw{e}{s}")
            rows = w1[e, s * K_PASS : (s + 1) * K_PASS, :].rearrange("(p j) h -> p j h", j=PACK)
            nc.sync.dma_start(out=w1_raw[e, s][:], in_=rows)

        def load_w2(e):
            w2_raw[e] = held([P, PACK, N], F32, f"w2_raw{e}")
            rows = w2[e].rearrange("(c a i b) n -> a c i (b n)", a=2, i=2, b=2)
            for a in range(2):
                nc.sync.dma_start(out=w2_raw[e][:, 2 * a : 2 * a + 2, :].rearrange("p b n -> p (b n)"), in_=rows[a])

        def load_list(name):
            tile, source = {"offs": (offs_sb, offs), "offs2": (offs2_sb, offs2), "pos0": (pos_sb[0], pos1), "pos1": (pos_sb[1], pos2)}[name]
            nc.sync.dma_start(tile[:], source)

        def load_gate():
            nc.sync.dma_start(out=gate_sb[:], in_=gate.rearrange("r p t -> p r t"))

        loaders = {"Llist": load_list, "Lfw": load_far_words, "Lfs": load_far_scales, "Lxo": load_xo, "Lw1": load_w1, "Lw2": load_w2, "Lgate": load_gate}
        for step in LOADS:
            loaders[step[0]](*step[1:])

        def cast(engine, target, source):
            if engine == "scalar":
                nc.scalar.copy(out=target, in_=source)
            elif engine == "vector":
                nc.vector.tensor_copy(out=target, in_=source)
            else:
                nc.gpsimd.tensor_scalar(target, source, 1.0, 0.0, MULT, ADD)

        tiles = {}

        def once(shape, dtype, name):
            if name not in tiles:
                tiles[name] = held(shape, dtype, name)
            return tiles[name]

        pairs, picked, own, far_w, far_s, first, second, h_banks, hidden, h_codes, sums = ({} for i in range(11))

        def cast_xo(s, u):
            w = 2 * s + u
            target = pair_words[:, w * T : (w + 1) * T].bitcast(BF16).rearrange("p (t j) -> p t j", j=2)
            cast(XO_ENGINE[2 * s + u], target, xo_raw[s, u][:].rearrange("p j t -> p t j"))

        def quantize(values, width, name):
            codes = held([P, width], U32, name + "_codes")
            scales = held([P, width], U8, name + "_scales")
            nc.vector.quantize_mx(out=codes[:].bitcast(FP8X4), scales=scales[:], in_=values)
            return codes, scales

        def expert_list(tile, e):
            return tile[:, 2 * e * LIST_COLS : 2 * (e + 1) * LIST_COLS]

        def pick_own(pair, s, u):
            picked = once([P, 2, 2 * C], U32, f"picked{2 * pair + s}")
            w = 2 * s + u
            window = pair_words[:, w * T : (w + 2) * T].bitcast(U32)
            nc.vector.tensor_copy(picked[:, u, :], window.indirect(expert_list(offs_sb, pair)))

        def group_own(k):
            grouped = once([P, 2 * C * PACK], BF16, f"own_grouped{k}")
            if k in GROUP_ON_SCALAR:
                nc.scalar.copy(
                    out=grouped[:].bitcast(F32).rearrange("p (c u) -> p c u", u=2),
                    in_=tiles[f"picked{k}"][:].bitcast(F32).rearrange("p u c -> p c u"),
                )
            else:
                nc.vector.tensor_copy(
                    out=grouped[:].bitcast(I32).rearrange("p (c u) -> p c u", u=2),
                    in_=tiles[f"picked{k}"][:].bitcast(I32).rearrange("p u c -> p c u"),
                )

        def quantize_own(k):
            own[k] = quantize(tiles[f"own_grouped{k}"][:], 2 * C, f"own{k}")

        def pick_far_words(pair, s):
            far_w[pair, s] = held([P, 2 * D], U32, f"far_w{pair}{s}")
            window = far_words[:, s * Q : (s + 2) * Q].bitcast(U32)
            nc.vector.tensor_copy(far_w[pair, s][:], window.indirect(expert_list(offs2_sb, pair)))

        def pick_far_scales(pair):
            far_s[pair] = held([P, 2 * D], U8, f"far_s{pair}")
            nc.vector.tensor_copy(far_s[pair][:], far_scales[:].bitcast(U8).indirect(expert_list(offs2_sb, pair)))

        def cast_w1(e, s, a):
            grouped = once([P, H * PACK], BF16, f"w1_grouped{e}{s}")
            target = grouped[:].rearrange("p (a b c i j) -> p a c j i b", a=2, b=2, i=2, j=PACK)
            source = w1_raw[e, s][:].rearrange("p j (c a i b) -> p a c j i b", a=2, i=2, b=2)
            engine = W1_ENGINE.get((e, s, a), "scalar")
            if engine == "gpsimd":
                for b in range(2):
                    cast(engine, target[:, a, :, :, :, b], source[:, a, :, :, :, b])
            else:
                cast(engine, target[:, a], source[:, a])

        def quantize_w1(e, s):
            first[e, s] = quantize(tiles[f"w1_grouped{e}{s}"][:], H, f"w1_{e}{s}")

        def cast_w2(e):
            grouped = once([P, N * PACK], BF16, f"w2_grouped{e}")
            cast(
                W2_ENGINE[e],
                grouped[:].rearrange("p (c i j) -> p c j i", i=4, j=PACK),
                w2_raw[e][:].rearrange("p j (c i) -> p c j i", i=4),
            )

        def quantize_w2(e):
            second[e] = quantize(tiles[f"w2_grouped{e}"][:], N, f"w2_{e}")

        def first_layer(kind, e, half):
            if kind == "own":
                tokens = [own[e // 2 * 2 + s] for s in range(PASSES)]
            else:
                tokens = [(far_w[e // 2, s][:], far_s[e // 2][4 * s : P, :]) for s in range(PASSES)]
            hidden = once([P, C, PACK], BF16, f"hidden_{kind}{e}")
            slots = slice(half * P, (half + 1) * P)
            in_pair = slice((e % 2) * C + half * P, (e % 2) * C + (half + 1) * P)
            bank = psum.tile([P, PACK, P], F32, name=f"h_{kind}", bufs=2 if kind == "own" else 2)
            for t in range(PACK):
                cols = slice(t * P, (t + 1) * P)
                for s in range(PASSES):
                    nc.tensor.matmul_mx(
                        out=bank[:, t, :],
                        lhsT=first[e, s][0][:, cols].bitcast(FP8X4),
                        lhsT_scale=first[e, s][1][:, cols],
                        rhs=tokens[s][0][:, in_pair].bitcast(FP8X4),
                        rhs_scale=tokens[s][1][:, in_pair],
                        start=(s == 0),
                        stop=(s == PASSES - 1),
                    )
            nc.scalar.activation(
                out=hidden[:, slots, :], in_=bank[:].rearrange("p t c -> p c t"), func=RELU, bias=no_bias[:]
            )

        def quantize_hidden(kind, e):
            hidden = tiles[f"hidden_{kind}{e}"]
            h_codes[kind, e] = quantize(hidden[:].rearrange("p c t -> p (c t)"), C, f"h_{kind}{e}")

        out_rows = out.rearrange("(nt p) c -> p nt c", p=P)
        slot_rows = [held([P, E * C], F32, f"slot_rows{nt}") for nt in range(N_TILES)]

        def second_layer(kind, e):
            codes, scales = h_codes[kind, e]
            bank = psum.tile([P, N_TILES, C], F32, name=f"y_{kind}", bufs=2 if kind == "own" else 2)
            for nt in range(N_TILES):
                cols = slice(nt * P, (nt + 1) * P)
                nc.tensor.matmul_mx(
                    out=bank[:, nt, :],
                    lhsT=second[e][0][:, cols].bitcast(FP8X4),
                    lhsT_scale=second[e][1][:, cols],
                    rhs=codes[:].bitcast(FP8X4),
                    rhs_scale=scales[:],
                    start=True,
                    stop=True,
                )
            if kind == "own":
                for nt in range(N_TILES):
                    nc.scalar.copy(out=slot_rows[nt][:, e * C : (e + 1) * C], in_=bank[:, nt, :])
            else:
                result = held([P, N_TILES, D], F32, f"far_result{e}")
                cast("vector" if e in Z_ON_VECTOR else "scalar", result[:], bank[:])
                nc.sync.dma_start(out=out_rows[:, :, T + e * D : T + (e + 1) * D], in_=result[:])

        parts = {}

        def weighted(nt, r):
            parts[nt, r] = held([P, T], F32, f"part{nt}{r}")
            nc.vector.tensor_tensor(parts[nt, r][:], slot_rows[nt][:].indirect(pos_sb[r][:]), gate_sb[:, r, :], MULT)

        def combine(nt):
            combined = held([P, T], F32, f"combined{nt}")
            nc.vector.tensor_tensor(combined[:], parts[nt, 0][:], parts[nt, 1][:], ADD)
            nc.sync.dma_start(out=out_rows[:, nt, 0:T], in_=combined[:])

        steps = {"cx": cast_xo, "og": pick_own, "il": group_own, "qo": quantize_own, "fw": pick_far_words, "fs": pick_far_scales,
                 "c1": cast_w1, "q1": quantize_w1, "c2": cast_w2, "q2": quantize_w2, "h": first_layer, "qh": quantize_hidden,
                 "y": second_layer, "cg": weighted, "add": combine}
        for step in ORDER:
            steps[step[0]](*step[1:])
